import numpy as np
import ml_dtypes


def mxq(x, axis, fmt="e4m3"):
    dtype, down = {"e4m3": (ml_dtypes.float8_e4m3fn, 7), "e5m2": (ml_dtypes.float8_e5m2, 14)}[fmt]
    v = np.moveaxis(np.asarray(x, np.float32).astype(ml_dtypes.bfloat16).astype(np.float64), axis, -1)
    blocks = v.reshape(v.shape[:-1] + (-1, 32))
    amax = np.abs(blocks).max(-1, keepdims=True)
    byte = np.maximum(np.where(amax > 0, np.frexp(amax)[1] - 1 + 127, 0) - down, 1)
    scale = np.exp2(byte - 127.0)
    codes = (blocks / scale).astype(np.float32).astype(dtype).astype(np.float64)
    return np.moveaxis((codes * scale).reshape(v.shape), -1, axis)


WIDE = False


def mx_kscale(k):
    if not WIDE:
        return np.ones(k)
    levels = np.array([10, -10, 5, -5, 0])
    if k % 512:
        return np.exp2(np.random.permutation(np.resize(levels, k // 32))).repeat(32)
    a = np.empty((k // 512, 16))
    for p in range(k // 512):
        a[p, :8] = np.random.permutation(np.resize(levels, 8))
        for g in range(8):
            far = levels[np.abs(levels - a[p, g]) >= 10]
            a[p, g + 8] = far[np.random.randint(len(far))]
    return np.exp2(a.ravel()).repeat(32)


def f64(x):
    return np.asarray(x).astype(np.float64)


def striped(idx):
    return np.tile(idx.reshape(-1, 16).T, (8, 1)).astype(np.uint16)


def unstriped(offs):
    return offs[:16].T.reshape(-1).astype(np.int64)


def striped8(idx):
    return np.concatenate([x.reshape(-1, 16).T for x in idx]).astype(np.uint16)


def runs(offs, k):
    lists = np.stack([offs[16 * r : 16 * r + 16].T.reshape(-1) for r in range(8)]).astype(np.int64)
    return lists[np.arange(k) % 512 // 64]


def pack_weight(w):
    k, n = w.shape
    w = f64(np.asarray(w, np.float32).astype(ml_dtypes.bfloat16)).reshape(k // 32, 32, n)
    amax = np.abs(w).max(1)
    byte = np.clip(np.where(amax > 0, np.frexp(amax)[1] - 1 + 127 - 7, 1), 1, 254)
    scaled = (w * np.exp2(127.0 - byte)[:, None, :]).reshape(k, n).astype(np.float32)
    words = np.ascontiguousarray(scaled.reshape(k // 512, 128, 4, n).transpose(0, 1, 3, 2)).astype(ml_dtypes.float8_e4m3fn).view(np.uint8)
    return words, np.ascontiguousarray(byte.astype(np.uint8).reshape(k // 512, 16, n))


def unpack_weight(words, scales):
    g, p, n, _ = words.shape
    vals = np.ascontiguousarray(words).view(ml_dtypes.float8_e4m3fn).astype(np.float64) * np.repeat(np.exp2(scales.astype(np.float64) - 127.0), 8, axis=1)[..., None]
    return vals.transpose(0, 1, 3, 2).reshape(g * 512, n)


def sigmoid(v):
    return 1.0 / (1.0 + np.exp(-np.maximum(v, -700.0)))

def planes(y):
    n, m = y.shape
    v = y.astype(np.float32).astype(ml_dtypes.bfloat16).astype(np.float64).reshape(n // 32, 32, m)
    top = np.abs(v).max(1)
    byte = np.clip(np.where(top > 0, np.frexp(top)[1] - 1 + 127 - 7, 1), 1, 254)
    codes = (v * np.exp2(127.0 - byte)[:, None, :]).reshape(n, m).astype(np.float32).astype(ml_dtypes.float8_e4m3fn).view(np.uint8)
    words = codes.reshape(n // 512, 128, 4, m).transpose(0, 1, 3, 2)
    return np.ascontiguousarray(words), np.ascontiguousarray(byte.astype(np.uint8).reshape(n // 512, 16, m))


K, T, S, V, H, J = 512, 2048, 512, 256, 512, 512


def setup_inputs():
    n = np.random.standard_normal
    s = mx_kscale(K)[:, None]
    u = mx_kscale(S)
    packed_xT = pack_weight(n((K, T)) * s)
    packed_w1 = pack_weight(n((K, H)) / np.sqrt(K) / s)
    packed_w2 = pack_weight(n((K, H)) / np.sqrt(K) / s)
    return {
        "x_words": packed_xT[0],
        "x_scales": packed_xT[1],
        "w1_words": packed_w1[0],
        "w1_scales": packed_w1[1],
        "w2_words": packed_w2[0],
        "w2_scales": packed_w2[1],
        "tab": n((H, J)).astype(np.float32),
        "ga": (np.random.uniform(0.5, 1.5, (H, 1)) * u[:, None]).astype(np.float32),
        "gb": (np.random.uniform(0.5, 1.5, (H, 1)) / u[:, None]).astype(np.float32),
        "offs": striped8(np.random.randint(0, T, (8, S))),
        "two": striped(np.random.permutation(T)[:V]),
        "n1": striped8(np.random.randint(0, J, (8, S))),
        "n2": striped8(np.random.randint(0, J, (8, S))),
        "n3": striped8(np.stack([np.random.permutation(S) for _ in range(8)])),
        "n4": striped(np.random.permutation(V)),
        "n5": striped(np.random.permutation(V)),
        "n6": striped(np.random.permutation(V)),
    }


def reference(x_words, x_scales, w1_words, w1_scales, w2_words, w2_scales, tab, ga, gb, offs, two, n1, n2, n3, n4, n5, n6):
    xq = unpack_weight(x_words, x_scales)[np.arange(K)[:, None], runs(offs, K)]
    a = unpack_weight(w1_words, w1_scales).T @ xq
    z = f64(ga) * ((a[np.arange(H)[:, None], runs(n3, H)]) * (f64(tab)[np.arange(H)[:, None], runs(n1, H)]) + f64(tab)[np.arange(H)[:, None], runs(n2, H)])
    x_two = unpack_weight(x_words, x_scales)[:, unstriped(two)]
    b = unpack_weight(w2_words, w2_scales).T @ x_two
    z2 = f64(gb) * (b - b[:, unstriped(n4)])
    s = 0.0625 * ((mxq(z, 0, "e4m3").T @ mxq(z2, 0, "e4m3")))
    st = s * (sigmoid(s[:, unstriped(n5)]))
    out_0 = st - st[:, unstriped(n6)]
    return (out_0,) + planes(out_0)

@@ -1,0 +1,217 @@
+from contextlib import ExitStack
+
+import concourse.mybir as mybir
+
+K, T, S, V, H, J = 512, 2048, 512, 256, 512, 512
+FLOPS = 2 * K * H * S + 2 * K * H * V + 2 * H * S * V
+
+F32 = mybir.dt.float32
+BF16 = mybir.dt.bfloat16
+U32 = mybir.dt.uint32
+I32 = mybir.dt.int32
+U16 = mybir.dt.uint16
+U8 = mybir.dt.uint8
+FP8X4 = mybir.dt.float8_e4m3fn_x4
+ALU = mybir.AluOpType
+ACT = mybir.ActivationFunctionType
+
+P = 128
+PACK = 4
+
+
+def tile_picked_hkqkindadifhopg_none_po_kernel(
+    tc, x_words, x_scales, w1_words, w1_scales, w2_words, w2_scales, tab, ga, gb,
+    offs, two, n1, n2, n3, n4, n5, n6, out_0, out_1, out_2,
+):
+    nc = tc.nc
+    with ExitStack() as ctx:
+        keep = ctx.enter_context(tc.tile_pool(name="keep", bufs=1))
+        psum = ctx.enter_context(tc.psum_pool(name="psum", bufs=1))
+
+        def sb(name, shape, dtype):
+            return keep.tile(shape, dtype, name=name, align_bytes=64)
+
+        def load_list(name, dram):
+            t = keep.tile([P, dram.shape[1]], U16, name=name)
+            nc.sync.dma_start(t[:], dram)
+            return t
+
+        def entries(lst, start, count):
+            return lst[:, start // 16 : (start + count) // 16]
+
+        def words_view(dram):
+            return dram[0].rearrange("p n t -> p (n t)").bitcast(I32)
+
+        xs = sb("xs", [P, T], U8)
+        xsc = sb("xsc", [P, S + V], U8)
+        ws = sb("ws", [P, H], U8)
+        nc.gpsimd.memset(xs[:].bitcast(I32), 0)
+        nc.vector.memset(ws[:].bitcast(I32), 0)
+        nc.vector.memset(xsc[:].bitcast(I32), 0)
+
+        tab_v = tab.rearrange("(p t) j -> p t j", t=PACK)
+        tabs = [sb(f"tab{t}", [P, J], F32) for t in range(PACK)]
+        tabg = [sb(f"tabg{t}", [P, J], F32) for t in range(PACK)]
+        xw = sb("xw", [P, T], U32)
+        w1 = sb("w1", [P, H], U32)
+        w2 = sb("w2", [P, H], U32)
+        ga_t = sb("ga_t", [P, PACK], F32)
+        gb_t = sb("gb_t", [P, PACK], F32)
+
+        l1 = load_list("l1", n1)
+        nc.sync.dma_start(tabs[0][:], tab_v[:, 0, :])
+        lo = load_list("lo", offs)
+        nc.sync.dma_start(xs[0:P:8, :].bitcast(I32), x_scales[0].bitcast(I32))
+        lt = load_list("lt", two)
+        nc.sync.dma_start(ga_t[:], ga.rearrange("(p t) o -> p (t o)", t=PACK))
+        l2 = load_list("l2", n2)
+        nc.sync.dma_start(xw[:].bitcast(I32), words_view(x_words))
+        nc.sync.dma_start(tabs[1][:], tab_v[:, 1, :])
+        nc.sync.dma_start(w1[:].bitcast(I32), words_view(w1_words))
+        for q in range(4):
+            nc.sync.dma_start(ws[32 * q : 32 * q + 4, :].bitcast(I32), w1_scales[0, 4 * q : 4 * q + 4, :].bitcast(I32))
+        for q in range(4):
+            nc.sync.dma_start(ws[32 * q + 4 : 32 * q + 8, :].bitcast(I32), w2_scales[0, 4 * q : 4 * q + 4, :].bitcast(I32))
+        nc.sync.dma_start(tabs[2][:], tab_v[:, 2, :])
+
+        xsg = sb("xsg", [P, S + V], U8)
+        nc.vector.tensor_copy(xsg[:, 0:S], xs[:].indirect(lo[:]))
+        nc.vector.tensor_copy(xsg[:, S : S + V], xs[:].indirect(lt[:]))
+        for q in range(4):
+            nc.sync.dma_start(xsc[32 * q : 32 * q + 4, :].bitcast(I32), xsg[32 * q : 32 * q + 32 : 8, :].bitcast(I32))
+
+        nc.sync.dma_start(tabs[3][:], tab_v[:, 3, :])
+        l3 = load_list("l3", n3)
+        nc.sync.dma_start(w2[:].bitcast(I32), words_view(w2_words))
+        nc.sync.dma_start(gb_t[:], gb.rearrange("(p t) o -> p (t o)", t=PACK))
+        l4 = load_list("l4", n4)
+        l5 = load_list("l5", n5)
+        l6 = load_list("l6", n6)
+
+        for t in range(PACK):
+            nc.gpsimd.tensor_scalar(tabg[t][:], tabs[t][:], ga_t[:, t : t + 1], 0.0, ALU.mult, ALU.add)
+
+        xg = sb("xg", [P, S], U32)
+        xg2 = sb("xg2", [P, V], U32)
+        nc.vector.tensor_copy(xg[:], xw[:].bitcast(U32).indirect(lo[:]))
+
+        w1d = sb("w1d", [P, H], U32)
+        w2d = sb("w2d", [P, H], U32)
+        wsd = sb("wsd", [P, H], U8)
+
+        def deal(dst, src):
+            nc.vector.tensor_copy(dst.rearrange("p (t m) -> p m t", t=PACK), src.rearrange("p (m t) -> p m t", t=PACK))
+
+        deal(w1d[:].bitcast(I32), w1[:].bitcast(I32))
+        deal(wsd[:], ws[:])
+
+        t1 = sb("t1", [P, PACK, S], F32)
+        t2 = sb("t2", [P, PACK, S], F32)
+        ag = sb("ag", [P, PACK, S], F32)
+        u = sb("u", [P, PACK, S], F32)
+        HS = S // 2
+
+        for t in range(PACK):
+            for h in range(2):
+                cols = slice(h * HS, (h + 1) * HS)
+                if t in (1, 2):
+                    nc.vector.tensor_copy(t1[:, t, cols], tabs[t][:].indirect(entries(l1, h * HS, HS)))
+                else:
+                    nc.scalar.activation(t1[:, t, cols], tabs[t][:].indirect(entries(l1, h * HS, HS)), ACT.Copy)
+            for h in range(2):
+                cols = slice(h * HS, (h + 1) * HS)
+                nc.scalar.activation(t2[:, t, cols], tabg[t][:].indirect(entries(l2, h * HS, HS)), ACT.Copy)
+
+        a_sb = [sb(f"a{t}", [P, S], F32) for t in range(PACK)]
+        for t in range(PACK):
+            acc = psum.tile([P, S], F32, name=f"acc_a{t}", tag=f"bank{t}")
+            cols = slice(P * t, P * (t + 1))
+            nc.tensor.matmul_mx(acc[:], w1d[:, cols].bitcast(FP8X4), wsd[:, cols], xg[:].bitcast(FP8X4), xsc[:, 0:S], start=True, stop=True)
+            nc.vector.tensor_scalar(a_sb[t][:], acc[:], ga_t[:, t : t + 1], None, ALU.mult)
+
+        nc.vector.tensor_copy(xg2[:], xw[:].bitcast(U32).indirect(lt[:]))
+        deal(w2d[:].bitcast(I32), w2[:].bitcast(I32))
+        b_sb = sb("b_sb", [P, PACK, V], F32)
+        for t in range(PACK):
+            acc = psum.tile([P, V], F32, name=f"acc_b{t}", tag=f"bank{4 + t}")
+            cols = slice(P * t, P * (t + 1))
+            nc.tensor.matmul_mx(acc[:], w2d[:, cols].bitcast(FP8X4), wsd[4:P, cols], xg2[:].bitcast(FP8X4), xsc[:, S : S + V], start=True, stop=True)
+            nc.vector.tensor_scalar(b_sb[:, t, :], acc[:], gb_t[:, t : t + 1], None, ALU.mult)
+
+        zb = sb("zb", [P, PACK, P, PACK], BF16)
+
+        def z_half(h):
+            cols = slice(h * HS, (h + 1) * HS)
+            for t in range(PACK):
+                nc.scalar.activation(ag[:, t, cols], a_sb[t][:].indirect(entries(l3, h * HS, HS)), ACT.Copy)
+                nc.vector.tensor_tensor(u[:, t, cols], ag[:, t, cols], t1[:, t, cols], ALU.mult)
+            m = slice(h * HS // PACK, (h + 1) * HS // PACK)
+            nc.vector.tensor_tensor(
+                zb[:, :, m, :].rearrange("p i c t -> p c t i"),
+                u[:, :, cols].rearrange("p t (c i) -> p c t i", i=PACK),
+                t2[:, :, cols].rearrange("p t (c i) -> p c t i", i=PACK),
+                ALU.add,
+            )
+
+        z_half(0)
+        z_half(1)
+        zc = sb("zc", [P, S], U32)
+        zs = sb("zs", [P, S], U8)
+        for i in range(PACK):
+            cols = slice(P * i, P * (i + 1))
+            nc.vector.quantize_mx(zc[:, cols].bitcast(FP8X4), zs[:, cols], zb[:, i, :, :].rearrange("p m t -> p (m t)"))
+
+        HV = V // 2
+        bg = sb("bg", [P, PACK, V], F32)
+        z2b = sb("z2b", [P, V, PACK], BF16)
+        z2c = sb("z2c", [P, V], U32)
+        z2s = sb("z2s", [P, V], U8)
+        for h in range(2):
+            cols = slice(h * HV, (h + 1) * HV)
+            for t in range(PACK):
+                nc.scalar.activation(bg[:, t, cols], b_sb[:, t, :].indirect(entries(l4, h * HV, HV)), ACT.Copy)
+            nc.vector.tensor_tensor(
+                z2b[:, cols, :].rearrange("p (c i) t -> p c t i", i=PACK),
+                b_sb[:, :, cols].rearrange("p t (c i) -> p c t i", i=PACK),
+                bg[:, :, cols].rearrange("p t (c i) -> p c t i", i=PACK),
+                ALU.subtract,
+            )
+            nc.vector.quantize_mx(z2c[:, cols].bitcast(FP8X4), z2s[:, cols], z2b[:, cols, :].rearrange("p v t -> p (v t)"))
+
+        s_sb = [sb(f"s{t}", [P, V], F32) for t in range(PACK)]
+        accs = []
+        for i in range(PACK):
+            cols = slice(P * i, P * (i + 1))
+            acc = psum.tile([P, V], F32, name=f"acc_s{i}", tag=f"bank{i}")
+            nc.tensor.matmul_mx(acc[:], zc[:, cols].bitcast(FP8X4), zs[:, cols], z2c[:].bitcast(FP8X4), z2s[:], start=True, stop=True)
+            accs.append(acc)
+        sg = sb("sg", [P, PACK, V], F32)
+        st = sb("st", [P, PACK, V], F32)
+        for i in range(PACK):
+            nc.vector.tensor_scalar(s_sb[i][:], accs[i][:], 0.0625, None, ALU.mult)
+            for h in range(2):
+                nc.scalar.activation(sg[:, i, h * HV : (h + 1) * HV], s_sb[i][:].indirect(entries(l5, h * HV, HV)), ACT.Sigmoid)
+        for i in range(PACK):
+            nc.vector.tensor_tensor(st[:, i, :], s_sb[i][:], sg[:, i, :], ALU.mult)
+
+        stg = sb("stg", [P, PACK, V], F32)
+        o = sb("o", [P, PACK, V], F32)
+        ob = sb("ob", [P, V, PACK], BF16)
+        oc = sb("oc", [P, V], U32)
+        osc = sb("osc", [P, V], U8)
+        out_v = out_0.rearrange("(p t) v -> p t v", t=PACK)
+        for c0, width in ((0, 128), (128, 64), (192, 64)):
+            cols = slice(c0, c0 + width)
+            for i in range(PACK):
+                nc.scalar.activation(stg[:, i, cols], st[:, i, :].indirect(entries(l6, c0, width)), ACT.Copy)
+            nc.vector.tensor_tensor(o[:, :, cols], st[:, :, cols], stg[:, :, cols], ALU.subtract)
+            nc.sync.dma_start(out_v[:, :, cols], o[:, :, cols])
+            nc.vector.tensor_copy(
+                ob[:, cols, :].rearrange("p (c i) t -> p c t i", i=PACK),
+                o[:, :, cols].rearrange("p t (c i) -> p c t i", i=PACK),
+            )
+            nc.vector.quantize_mx(oc[:, cols].bitcast(FP8X4), osc[:, cols], ob[:, cols, :].rearrange("p v t -> p (v t)"))
+            nc.sync.dma_start(words_view(out_1)[:, cols], oc[:, cols].bitcast(I32))
+        for q in range(4):
+            eng = nc.scalar if q % 2 else nc.sync
+            eng.dma_start(out_2[0, 4 * q : 4 * q + 4, :].bitcast(I32), osc[32 * q : 32 * q + 4, :].bitcast(I32))

@@ -42,6 +42,11 @@ def tile_picked_hkqkindadifhopg_none_po_kernel(
         def words_view(dram):
             return dram[0].rearrange("p n t -> p (n t)").bitcast(I32)
 
+        warm_in = sb("warm_in", [P, 1], F32)
+        warm_out = sb("warm_out", [P, 1], F32)
+        nc.vector.memset(warm_in[:], 0.0)
+        nc.scalar.activation(warm_out[:], warm_in[:], ACT.Sigmoid)
+
         xs = sb("xs", [P, T], U8)
         xsc = sb("xsc", [P, S + V], U8)
         ws = sb("ws", [P, H], U8)

@@ -17,6 +17,8 @@ ACT = mybir.ActivationFunctionType
 
 P = 128
 PACK = 4
+HS = S // 2
+HV = V // 2
 
 
 def tile_picked_hkqkindadifhopg_none_po_kernel(
@@ -28,8 +30,8 @@ def tile_picked_hkqkindadifhopg_none_po_kernel(
         keep = ctx.enter_context(tc.tile_pool(name="keep", bufs=1))
         psum = ctx.enter_context(tc.psum_pool(name="psum", bufs=1))
 
-        def sb(name, shape, dtype):
-            return keep.tile(shape, dtype, name=name, align_bytes=64)
+        def sb(name, shape, dtype, tag=None):
+            return keep.tile(shape, dtype, name=name, tag=tag or name, align_bytes=64)
 
         def load_list(name, dram):
             t = keep.tile([P, dram.shape[1]], U16, name=name)
@@ -42,17 +44,13 @@ def tile_picked_hkqkindadifhopg_none_po_kernel(
         def words_view(dram):
             return dram[0].rearrange("p n t -> p (n t)").bitcast(I32)
 
-        warm_in = sb("warm_in", [P, 1], F32)
-        warm_out = sb("warm_out", [P, 1], F32)
-        nc.vector.memset(warm_in[:], 0.0)
-        nc.scalar.activation(warm_out[:], warm_in[:], ACT.Sigmoid)
+        def deal(dst, src):
+            nc.vector.tensor_copy(dst.rearrange("p (t m) -> p m t", t=PACK), src.rearrange("p (m t) -> p m t", t=PACK))
 
         xs = sb("xs", [P, T], U8)
-        xsc = sb("xsc", [P, S + V], U8)
-        ws = sb("ws", [P, H], U8)
+        ws = sb("ws", [P, 2, H], U8)
         nc.gpsimd.memset(xs[:].bitcast(I32), 0)
         nc.vector.memset(ws[:].bitcast(I32), 0)
-        nc.vector.memset(xsc[:].bitcast(I32), 0)
 
         tab_v = tab.rearrange("(p t) j -> p t j", t=PACK)
         tabs = [sb(f"tab{t}", [P, J], F32) for t in range(PACK)]
@@ -62,138 +60,144 @@ def tile_picked_hkqkindadifhopg_none_po_kernel(
         w2 = sb("w2", [P, H], U32)
         ga_t = sb("ga_t", [P, PACK], F32)
         gb_t = sb("gb_t", [P, PACK], F32)
-
-        l1 = load_list("l1", n1)
-        nc.sync.dma_start(tabs[0][:], tab_v[:, 0, :])
-        lo = load_list("lo", offs)
-        nc.sync.dma_start(xs[0:P:8, :].bitcast(I32), x_scales[0].bitcast(I32))
-        lt = load_list("lt", two)
-        nc.sync.dma_start(ga_t[:], ga.rearrange("(p t) o -> p (t o)", t=PACK))
-        l2 = load_list("l2", n2)
-        nc.sync.dma_start(xw[:].bitcast(I32), words_view(x_words))
-        nc.sync.dma_start(tabs[1][:], tab_v[:, 1, :])
-        nc.sync.dma_start(w1[:].bitcast(I32), words_view(w1_words))
-        for q in range(4):
-            nc.sync.dma_start(ws[32 * q : 32 * q + 4, :].bitcast(I32), w1_scales[0, 4 * q : 4 * q + 4, :].bitcast(I32))
-        for q in range(4):
-            nc.sync.dma_start(ws[32 * q + 4 : 32 * q + 8, :].bitcast(I32), w2_scales[0, 4 * q : 4 * q + 4, :].bitcast(I32))
-        nc.sync.dma_start(tabs[2][:], tab_v[:, 2, :])
-
         xsg = sb("xsg", [P, S + V], U8)
-        nc.vector.tensor_copy(xsg[:, 0:S], xs[:].indirect(lo[:]))
-        nc.vector.tensor_copy(xsg[:, S : S + V], xs[:].indirect(lt[:]))
-        for q in range(4):
-            nc.sync.dma_start(xsc[32 * q : 32 * q + 4, :].bitcast(I32), xsg[32 * q : 32 * q + 32 : 8, :].bitcast(I32))
+        xsc = sb("xsc", [P, S + V], U8)
+        xg = sb("xg", [P, S], U32)
+        xg2 = sb("xg2", [P, V], U32)
+        w1d = sb("w1d", [P, H], U32)
+        w2d = sb("w2d", [P, H], U32)
+        wsc = sb("wsc", [P, 2, H], U8)
+        t1 = sb("t1", [P, PACK, S], F32)
+        t2 = [sb(f"t2_{h}", [P, PACK, HS], F32) for h in range(2)]
+        u = sb("u", [P, PACK, HS], F32)
 
-        nc.sync.dma_start(tabs[3][:], tab_v[:, 3, :])
+        def load_tab(t):
+            nc.sync.dma_start(tabs[t][:], tab_v[:, t, :])
+
+        def load_ws(first, dram):
+            nc.sync.dma_start(ws[0:P:8, first, :].bitcast(I32), dram[0].bitcast(I32))
+
+        def fetch(dst, window, lst, t, h, on_vector):
+            if on_vector:
+                nc.vector.tensor_copy(dst, window[t][:].indirect(entries(lst, h * HS, HS)))
+            else:
+                nc.scalar.activation(dst, window[t][:].indirect(entries(lst, h * HS, HS)), ACT.Copy)
+
+        def product(name, bank, t, wd, first, rhs, rhs_scale, dst, gain):
+            acc = psum.tile([P, rhs.shape[1]], F32, name=f"acc_{name}{t}", tag=f"bank{bank}")
+            cols = slice(P * t, P * (t + 1))
+            nc.tensor.matmul_mx(acc[:], wd[:, cols].bitcast(FP8X4), wsc[:, first, cols], rhs.bitcast(FP8X4), rhs_scale, start=True, stop=True)
+            nc.vector.tensor_scalar(dst, acc[:], gain[:, t : t + 1], None, ALU.mult)
+
+        nc.gpsimd.dma_start(ga_t[:], ga.rearrange("(p t) o -> p (t o)", t=PACK))
+        nc.gpsimd.dma_start(gb_t[:], gb.rearrange("(p t) o -> p (t o)", t=PACK))
+        l1 = load_list("l1", n1)
+        load_tab(0)
+        nc.sync.dma_start(xs[0:P:8, :].bitcast(I32), x_scales[0].bitcast(I32))
+        lo = load_list("lo", offs)
+        lt = load_list("lt", two)
+        load_ws(0, w1_scales)
+        load_ws(1, w2_scales)
+        nc.sync.dma_start(xw[:].bitcast(I32), words_view(x_words))
+        l2 = load_list("l2", n2)
         l3 = load_list("l3", n3)
-        nc.sync.dma_start(w2[:].bitcast(I32), words_view(w2_words))
-        nc.sync.dma_start(gb_t[:], gb.rearrange("(p t) o -> p (t o)", t=PACK))
         l4 = load_list("l4", n4)
         l5 = load_list("l5", n5)
         l6 = load_list("l6", n6)
+        nc.sync.dma_start(w1[:].bitcast(I32), words_view(w1_words))
+        load_tab(1)
+        load_tab(2)
+        nc.vector.tensor_copy(xsg[:, 0:S], xs[:].indirect(lo[:]))
+        nc.vector.tensor_copy(xsg[:, S : S + V], xs[:].indirect(lt[:]))
+        nc.vector.tensor_copy(xsc[:].bitcast(I32), xsg[:].bitcast(I32))
+        for r in range(1, 4):
+            nc.sync.dma_start(xsc[r:P:32, :].bitcast(I32), xsg[8 * r : P : 32, :].bitcast(I32))
+        nc.vector.tensor_copy(wsc[:].rearrange("p w (t m) -> p w m t", t=PACK), ws[:].rearrange("p w (m t) -> p w m t", t=PACK))
+        for r in range(1, 4):
+            nc.sync.dma_start(wsc[r:P:32].bitcast(I32), wsc[8 * r : P : 32].bitcast(I32))
+        nc.sync.dma_start(w2[:].bitcast(I32), words_view(w2_words))
+        load_tab(3)
 
         for t in range(PACK):
             nc.gpsimd.tensor_scalar(tabg[t][:], tabs[t][:], ga_t[:, t : t + 1], 0.0, ALU.mult, ALU.add)
-
-        xg = sb("xg", [P, S], U32)
-        xg2 = sb("xg2", [P, V], U32)
         nc.vector.tensor_copy(xg[:], xw[:].bitcast(U32).indirect(lo[:]))
-
-        w1d = sb("w1d", [P, H], U32)
-        w2d = sb("w2d", [P, H], U32)
-        wsd = sb("wsd", [P, H], U8)
-
-        def deal(dst, src):
-            nc.vector.tensor_copy(dst.rearrange("p (t m) -> p m t", t=PACK), src.rearrange("p (m t) -> p m t", t=PACK))
-
         deal(w1d[:].bitcast(I32), w1[:].bitcast(I32))
-        deal(wsd[:], ws[:])
+        nc.vector.tensor_copy(xg2[:], xw[:].bitcast(U32).indirect(lt[:]))
+        deal(w2d[:].bitcast(I32), w2[:].bitcast(I32))
 
-        t1 = sb("t1", [P, PACK, S], F32)
-        t2 = sb("t2", [P, PACK, S], F32)
-        ag = sb("ag", [P, PACK, S], F32)
-        u = sb("u", [P, PACK, S], F32)
-        HS = S // 2
-
+        on_vector = ((2, 0), (3, 0), (3, 1))
         for t in range(PACK):
             for h in range(2):
-                cols = slice(h * HS, (h + 1) * HS)
-                if t in (1, 2):
-                    nc.vector.tensor_copy(t1[:, t, cols], tabs[t][:].indirect(entries(l1, h * HS, HS)))
-                else:
-                    nc.scalar.activation(t1[:, t, cols], tabs[t][:].indirect(entries(l1, h * HS, HS)), ACT.Copy)
+                if (t, h) not in on_vector:
+                    fetch(t1[:, t, h * HS : (h + 1) * HS], tabs, l1, t, h, False)
             for h in range(2):
-                cols = slice(h * HS, (h + 1) * HS)
-                nc.scalar.activation(t2[:, t, cols], tabg[t][:].indirect(entries(l2, h * HS, HS)), ACT.Copy)
+                fetch(t2[h][:, t, :], tabg, l2, t, h, False)
 
         a_sb = [sb(f"a{t}", [P, S], F32) for t in range(PACK)]
         for t in range(PACK):
-            acc = psum.tile([P, S], F32, name=f"acc_a{t}", tag=f"bank{t}")
-            cols = slice(P * t, P * (t + 1))
-            nc.tensor.matmul_mx(acc[:], w1d[:, cols].bitcast(FP8X4), wsd[:, cols], xg[:].bitcast(FP8X4), xsc[:, 0:S], start=True, stop=True)
-            nc.vector.tensor_scalar(a_sb[t][:], acc[:], ga_t[:, t : t + 1], None, ALU.mult)
-
-        nc.vector.tensor_copy(xg2[:], xw[:].bitcast(U32).indirect(lt[:]))
-        deal(w2d[:].bitcast(I32), w2[:].bitcast(I32))
+            product("a", t, t, w1d, 0, xg[:], xsc[:, 0:S], a_sb[t][:], ga_t)
         b_sb = sb("b_sb", [P, PACK, V], F32)
         for t in range(PACK):
-            acc = psum.tile([P, V], F32, name=f"acc_b{t}", tag=f"bank{4 + t}")
-            cols = slice(P * t, P * (t + 1))
-            nc.tensor.matmul_mx(acc[:], w2d[:, cols].bitcast(FP8X4), wsd[4:P, cols], xg2[:].bitcast(FP8X4), xsc[:, S : S + V], start=True, stop=True)
-            nc.vector.tensor_scalar(b_sb[:, t, :], acc[:], gb_t[:, t : t + 1], None, ALU.mult)
+            product("b", 4 + t, t, w2d, 1, xg2[:], xsc[:, S : S + V], b_sb[:, t, :], gb_t)
+        for t, h in on_vector:
+            fetch(t1[:, t, h * HS : (h + 1) * HS], tabs, l1, t, h, True)
 
         zb = sb("zb", [P, PACK, P, PACK], BF16)
 
-        def z_half(h):
-            cols = slice(h * HS, (h + 1) * HS)
+        def z_piece(c0, width, tag):
+            cols = slice(c0, c0 + width)
+            ag = sb(f"ag{c0}", [P, PACK, width], F32, tag=tag)
             for t in range(PACK):
-                nc.scalar.activation(ag[:, t, cols], a_sb[t][:].indirect(entries(l3, h * HS, HS)), ACT.Copy)
-                nc.vector.tensor_tensor(u[:, t, cols], ag[:, t, cols], t1[:, t, cols], ALU.mult)
-            m = slice(h * HS // PACK, (h + 1) * HS // PACK)
+                nc.scalar.activation(ag[:, t, :], a_sb[t][:].indirect(entries(l3, c0, width)), ACT.Copy)
+                if t % 2:
+                    nc.vector.tensor_tensor(u[:, t - 1 : t + 1, 0:width], ag[:, t - 1 : t + 1, :], t1[:, t - 1 : t + 1, cols], ALU.mult)
+            m = slice(c0 // PACK, (c0 + width) // PACK)
             nc.vector.tensor_tensor(
                 zb[:, :, m, :].rearrange("p i c t -> p c t i"),
-                u[:, :, cols].rearrange("p t (c i) -> p c t i", i=PACK),
-                t2[:, :, cols].rearrange("p t (c i) -> p c t i", i=PACK),
+                u[:, :, 0:width].rearrange("p t (c i) -> p c t i", i=PACK),
+                t2[c0 // HS][:, :, c0 % HS : c0 % HS + width].rearrange("p t (c i) -> p c t i", i=PACK),
                 ALU.add,
             )
 
-        z_half(0)
-        z_half(1)
+        def z2_all():
+            z2b = sb("z2b", [P, V, PACK], BF16, tag="u")
+            for h in range(2):
+                cols = slice(h * HV, (h + 1) * HV)
+                for t in range(PACK):
+                    nc.scalar.activation(bg[:, t, cols], b_sb[:, t, :].indirect(entries(l4, h * HV, HV)), ACT.Copy)
+                nc.vector.tensor_tensor(
+                    z2b[:, cols, :].rearrange("p (c i) t -> p c t i", i=PACK),
+                    b_sb[:, :, cols].rearrange("p t (c i) -> p c t i", i=PACK),
+                    bg[:, :, cols].rearrange("p t (c i) -> p c t i", i=PACK),
+                    ALU.subtract,
+                )
+                nc.vector.quantize_mx(z2c[:, cols].bitcast(FP8X4), z2s[:, cols], z2b[:, cols, :].rearrange("p v t -> p (v t)"))
+
         zc = sb("zc", [P, S], U32)
         zs = sb("zs", [P, S], U8)
-        for i in range(PACK):
-            cols = slice(P * i, P * (i + 1))
-            nc.vector.quantize_mx(zc[:, cols].bitcast(FP8X4), zs[:, cols], zb[:, i, :, :].rearrange("p m t -> p (m t)"))
 
-        HV = V // 2
+        def z_quant(n):
+            for i in range(0, PACK, n):
+                cols = slice(P * i, P * (i + n))
+                nc.vector.quantize_mx(zc[:, cols].bitcast(FP8X4), zs[:, cols], zb[:, i : i + n, :, :].rearrange("p i m t -> p (i m t)"))
+
         bg = sb("bg", [P, PACK, V], F32)
-        z2b = sb("z2b", [P, V, PACK], BF16)
         z2c = sb("z2c", [P, V], U32)
         z2s = sb("z2s", [P, V], U8)
-        for h in range(2):
-            cols = slice(h * HV, (h + 1) * HV)
-            for t in range(PACK):
-                nc.scalar.activation(bg[:, t, cols], b_sb[:, t, :].indirect(entries(l4, h * HV, HV)), ACT.Copy)
-            nc.vector.tensor_tensor(
-                z2b[:, cols, :].rearrange("p (c i) t -> p c t i", i=PACK),
-                b_sb[:, :, cols].rearrange("p t (c i) -> p c t i", i=PACK),
-                bg[:, :, cols].rearrange("p t (c i) -> p c t i", i=PACK),
-                ALU.subtract,
-            )
-            nc.vector.quantize_mx(z2c[:, cols].bitcast(FP8X4), z2s[:, cols], z2b[:, cols, :].rearrange("p v t -> p (v t)"))
+        z_piece(0, 256, None)
+        z_piece(256, 256, "ga_t")
+        z_quant(4)
+        z2_all()
 
         s_sb = [sb(f"s{t}", [P, V], F32) for t in range(PACK)]
-        accs = []
         for i in range(PACK):
             cols = slice(P * i, P * (i + 1))
-            acc = psum.tile([P, V], F32, name=f"acc_s{i}", tag=f"bank{i}")
+            acc = psum.tile([P, V], F32, name=f"acc_s{i}", tag=f"bank{4 + i}")
             nc.tensor.matmul_mx(acc[:], zc[:, cols].bitcast(FP8X4), zs[:, cols], z2c[:].bitcast(FP8X4), z2s[:], start=True, stop=True)
-            accs.append(acc)
+            nc.vector.tensor_scalar(s_sb[i][:], acc[:], 0.0625, None, ALU.mult)
         sg = sb("sg", [P, PACK, V], F32)
         st = sb("st", [P, PACK, V], F32)
         for i in range(PACK):
-            nc.vector.tensor_scalar(s_sb[i][:], accs[i][:], 0.0625, None, ALU.mult)
             for h in range(2):
                 nc.scalar.activation(sg[:, i, h * HV : (h + 1) * HV], s_sb[i][:].indirect(entries(l5, h * HV, HV)), ACT.Sigmoid)
         for i in range(PACK):
@@ -205,18 +209,21 @@ def tile_picked_hkqkindadifhopg_none_po_kernel(
         oc = sb("oc", [P, V], U32)
         osc = sb("osc", [P, V], U8)
         out_v = out_0.rearrange("(p t) v -> p t v", t=PACK)
-        for c0, width in ((0, 128), (128, 64), (192, 64)):
-            cols = slice(c0, c0 + width)
-            for i in range(PACK):
-                nc.scalar.activation(stg[:, i, cols], st[:, i, :].indirect(entries(l6, c0, width)), ACT.Copy)
-            nc.vector.tensor_tensor(o[:, :, cols], st[:, :, cols], stg[:, :, cols], ALU.subtract)
-            nc.sync.dma_start(out_v[:, :, cols], o[:, :, cols])
+        halves = [slice(0, HV), slice(HV, V)]
+        for i in range(PACK):
+            for h in range(2):
+                nc.scalar.activation(stg[:, i, halves[h]], st[:, i, :].indirect(entries(l6, h * HV, HV)), ACT.Copy)
+            for cols in (halves if i == PACK - 1 else [slice(0, V)]):
+                nc.vector.tensor_tensor(o[:, i, cols], st[:, i, cols], stg[:, i, cols], ALU.subtract)
+            nc.sync.dma_start(out_v[:, i, :], o[:, i, :])
+        for cols in halves:
             nc.vector.tensor_copy(
                 ob[:, cols, :].rearrange("p (c i) t -> p c t i", i=PACK),
                 o[:, :, cols].rearrange("p t (c i) -> p c t i", i=PACK),
             )
+        for cols in halves:
             nc.vector.quantize_mx(oc[:, cols].bitcast(FP8X4), osc[:, cols], ob[:, cols, :].rearrange("p v t -> p (v t)"))
-            nc.sync.dma_start(words_view(out_1)[:, cols], oc[:, cols].bitcast(I32))
+        nc.sync.dma_start(words_view(out_1), oc[:].bitcast(I32))
         for q in range(4):
-            eng = nc.scalar if q % 2 else nc.sync
+            eng = nc.sync if q == 3 else nc.scalar
             eng.dma_start(out_2[0, 4 * q : 4 * q + 4, :].bitcast(I32), osc[32 * q : 32 * q + 4, :].bitcast(I32))

@@ -60,8 +60,10 @@ def tile_picked_hkqkindadifhopg_none_po_kernel(
         w2 = sb("w2", [P, H], U32)
         ga_t = sb("ga_t", [P, PACK], F32)
         gb_t = sb("gb_t", [P, PACK], F32)
-        xsg = sb("xsg", [P, S + V], U8)
-        xsc = sb("xsc", [P, S + V], U8)
+        xsg = sb("xsg", [P, S], U8)
+        xsg2 = sb("xsg2", [P, V], U8)
+        xsc = sb("xsc", [P, S], U8)
+        xsc2 = sb("xsc2", [P, V], U8)
         xg = sb("xg", [P, S], U32)
         xg2 = sb("xg2", [P, V], U32)
         w1d = sb("w1d", [P, H], U32)
@@ -69,7 +71,11 @@ def tile_picked_hkqkindadifhopg_none_po_kernel(
         wsc = sb("wsc", [P, 2, H], U8)
         t1 = sb("t1", [P, PACK, S], F32)
         t2 = [sb(f"t2_{h}", [P, PACK, HS], F32) for h in range(2)]
-        u = sb("u", [P, PACK, HS], F32)
+
+        def place_rows(dst, src):
+            nc.vector.tensor_copy(dst[:].bitcast(I32), src[:].bitcast(I32))
+            for r in range(1, 4):
+                nc.sync.dma_start(dst[r:P:32, :].bitcast(I32), src[8 * r : P : 32, :].bitcast(I32))
 
         def load_tab(t):
             nc.sync.dma_start(tabs[t][:], tab_v[:, t, :])
@@ -89,43 +95,42 @@ def tile_picked_hkqkindadifhopg_none_po_kernel(
             nc.tensor.matmul_mx(acc[:], wd[:, cols].bitcast(FP8X4), wsc[:, first, cols], rhs.bitcast(FP8X4), rhs_scale, start=True, stop=True)
             nc.vector.tensor_scalar(dst, acc[:], gain[:, t : t + 1], None, ALU.mult)
 
-        nc.gpsimd.dma_start(ga_t[:], ga.rearrange("(p t) o -> p (t o)", t=PACK))
         nc.gpsimd.dma_start(gb_t[:], gb.rearrange("(p t) o -> p (t o)", t=PACK))
         l1 = load_list("l1", n1)
         load_tab(0)
         nc.sync.dma_start(xs[0:P:8, :].bitcast(I32), x_scales[0].bitcast(I32))
         lo = load_list("lo", offs)
-        lt = load_list("lt", two)
+        nc.sync.dma_start(ga_t[:], ga.rearrange("(p t) o -> p (t o)", t=PACK))
         load_ws(0, w1_scales)
         load_ws(1, w2_scales)
         nc.sync.dma_start(xw[:].bitcast(I32), words_view(x_words))
         l2 = load_list("l2", n2)
+        lt = load_list("lt", two)
         l3 = load_list("l3", n3)
         l4 = load_list("l4", n4)
-        l5 = load_list("l5", n5)
-        l6 = load_list("l6", n6)
-        nc.sync.dma_start(w1[:].bitcast(I32), words_view(w1_words))
         load_tab(1)
+        nc.sync.dma_start(w1[:].bitcast(I32), words_view(w1_words))
         load_tab(2)
-        nc.vector.tensor_copy(xsg[:, 0:S], xs[:].indirect(lo[:]))
-        nc.vector.tensor_copy(xsg[:, S : S + V], xs[:].indirect(lt[:]))
-        nc.vector.tensor_copy(xsc[:].bitcast(I32), xsg[:].bitcast(I32))
-        for r in range(1, 4):
-            nc.sync.dma_start(xsc[r:P:32, :].bitcast(I32), xsg[8 * r : P : 32, :].bitcast(I32))
+        load_tab(3)
+        nc.vector.tensor_copy(xsg[:], xs[:].indirect(lo[:]))
+        place_rows(xsc, xsg)
         nc.vector.tensor_copy(wsc[:].rearrange("p w (t m) -> p w m t", t=PACK), ws[:].rearrange("p w (m t) -> p w m t", t=PACK))
         for r in range(1, 4):
             nc.sync.dma_start(wsc[r:P:32].bitcast(I32), wsc[8 * r : P : 32].bitcast(I32))
         nc.sync.dma_start(w2[:].bitcast(I32), words_view(w2_words))
-        load_tab(3)
+        l5 = load_list("l5", n5)
+        l6 = load_list("l6", n6)
 
         for t in range(PACK):
             nc.gpsimd.tensor_scalar(tabg[t][:], tabs[t][:], ga_t[:, t : t + 1], 0.0, ALU.mult, ALU.add)
         nc.vector.tensor_copy(xg[:], xw[:].bitcast(U32).indirect(lo[:]))
         deal(w1d[:].bitcast(I32), w1[:].bitcast(I32))
+        nc.vector.tensor_copy(xsg2[:], xs[:].indirect(lt[:]))
+        place_rows(xsc2, xsg2)
         nc.vector.tensor_copy(xg2[:], xw[:].bitcast(U32).indirect(lt[:]))
         deal(w2d[:].bitcast(I32), w2[:].bitcast(I32))
 
-        on_vector = ((2, 0), (3, 0), (3, 1))
+        on_vector = ((1, 0), (2, 0), (3, 0))
         for t in range(PACK):
             for h in range(2):
                 if (t, h) not in on_vector:
@@ -135,13 +140,14 @@ def tile_picked_hkqkindadifhopg_none_po_kernel(
 
         a_sb = [sb(f"a{t}", [P, S], F32) for t in range(PACK)]
         for t in range(PACK):
-            product("a", t, t, w1d, 0, xg[:], xsc[:, 0:S], a_sb[t][:], ga_t)
+            product("a", t, t, w1d, 0, xg[:], xsc[:], a_sb[t][:], ga_t)
         b_sb = sb("b_sb", [P, PACK, V], F32)
         for t in range(PACK):
-            product("b", 4 + t, t, w2d, 1, xg2[:], xsc[:, S : S + V], b_sb[:, t, :], gb_t)
+            product("b", 4 + t, t, w2d, 1, xg2[:], xsc2[:], b_sb[:, t, :], gb_t)
         for t, h in on_vector:
             fetch(t1[:, t, h * HS : (h + 1) * HS], tabs, l1, t, h, True)
 
+        u = sb("u", [P, PACK, HS], F32, tag="gb_t")
         zb = sb("zb", [P, PACK, P, PACK], BF16)
 
         def z_piece(c0, width, tag):
@@ -160,7 +166,7 @@ def tile_picked_hkqkindadifhopg_none_po_kernel(
             )
 
         def z2_all():
-            z2b = sb("z2b", [P, V, PACK], BF16, tag="u")
+            z2b = sb("z2b", [P, V, PACK], BF16, tag="gb_t")
             for h in range(2):
                 cols = slice(h * HV, (h + 1) * HV)
                 for t in range(PACK):

from contextlib import ExitStack

import concourse.mybir as mybir

K, T, S, V, H, J = 512, 2048, 512, 256, 512, 512
FLOPS = 2 * K * H * S + 2 * K * H * V + 2 * H * S * V

F32 = mybir.dt.float32
BF16 = mybir.dt.bfloat16
U32 = mybir.dt.uint32
I32 = mybir.dt.int32
U16 = mybir.dt.uint16
U8 = mybir.dt.uint8
FP8X4 = mybir.dt.float8_e4m3fn_x4
ALU = mybir.AluOpType
ACT = mybir.ActivationFunctionType

P = 128
PACK = 4
HS = S // 2
HV = V // 2


def tile_picked_hkqkindadifhopg_none_po_kernel(
    tc, x_words, x_scales, w1_words, w1_scales, w2_words, w2_scales, tab, ga, gb,
    offs, two, n1, n2, n3, n4, n5, n6, out_0, out_1, out_2,
):
    nc = tc.nc
    with ExitStack() as ctx:
        keep = ctx.enter_context(tc.tile_pool(name="keep", bufs=1))
        psum = ctx.enter_context(tc.psum_pool(name="psum", bufs=1))

        def sb(name, shape, dtype, tag=None):
            return keep.tile(shape, dtype, name=name, tag=tag or name, align_bytes=64)

        def load_list(name, dram):
            t = keep.tile([P, dram.shape[1]], U16, name=name)
            nc.sync.dma_start(t[:], dram)
            return t

        def entries(lst, start, count):
            return lst[:, start // 16 : (start + count) // 16]

        def words_view(dram):
            return dram[0].rearrange("p n t -> p (n t)").bitcast(I32)

        def deal(dst, src):
            nc.vector.tensor_copy(dst.rearrange("p (t m) -> p m t", t=PACK), src.rearrange("p (m t) -> p m t", t=PACK))

        xs = sb("xs", [P, T], U8)
        ws = sb("ws", [P, 2, H], U8)
        nc.gpsimd.memset(xs[:].bitcast(I32), 0)
        nc.vector.memset(ws[:].bitcast(I32), 0)

        tab_v = tab.rearrange("(p t) j -> p t j", t=PACK)
        tabs = [sb(f"tab{t}", [P, J], F32) for t in range(PACK)]
        tabg = [sb(f"tabg{t}", [P, J], F32) for t in range(PACK)]
        xw = sb("xw", [P, T], U32)
        w1 = sb("w1", [P, H], U32)
        w2 = sb("w2", [P, H], U32)
        ga_t = sb("ga_t", [P, PACK], F32)
        gb_t = sb("gb_t", [P, PACK], F32)
        xsg = sb("xsg", [P, S], U8)
        xsg2 = sb("xsg2", [P, V], U8)
        xsc = sb("xsc", [P, S], U8)
        xsc2 = sb("xsc2", [P, V], U8)
        xg = sb("xg", [P, S], U32)
        xg2 = sb("xg2", [P, V], U32)
        w1d = sb("w1d", [P, H], U32)
        w2d = sb("w2d", [P, H], U32)
        wsc = sb("wsc", [P, 2, H], U8)
        t1 = sb("t1", [P, PACK, S], F32)
        t2 = [sb(f"t2_{h}", [P, PACK, HS], F32) for h in range(2)]

        def place_rows(dst, src):
            nc.vector.tensor_copy(dst[:].bitcast(I32), src[:].bitcast(I32))
            for r in range(1, 4):
                nc.sync.dma_start(dst[r:P:32, :].bitcast(I32), src[8 * r : P : 32, :].bitcast(I32))

        def load_tab(t):
            nc.sync.dma_start(tabs[t][:], tab_v[:, t, :])

        def load_ws(first, dram):
            nc.sync.dma_start(ws[0:P:8, first, :].bitcast(I32), dram[0].bitcast(I32))

        def fetch(dst, window, lst, t, h, on_vector):
            if on_vector:
                nc.vector.tensor_copy(dst, window[t][:].indirect(entries(lst, h * HS, HS)))
            else:
                nc.scalar.activation(dst, window[t][:].indirect(entries(lst, h * HS, HS)), ACT.Copy)

        def product(name, bank, t, wd, first, rhs, rhs_scale, dst, gain):
            acc = psum.tile([P, rhs.shape[1]], F32, name=f"acc_{name}{t}", tag=f"bank{bank}")
            cols = slice(P * t, P * (t + 1))
            nc.tensor.matmul_mx(acc[:], wd[:, cols].bitcast(FP8X4), wsc[:, first, cols], rhs.bitcast(FP8X4), rhs_scale, start=True, stop=True)
            nc.vector.tensor_scalar(dst, acc[:], gain[:, t : t + 1], None, ALU.mult)

        nc.gpsimd.dma_start(gb_t[:], gb.rearrange("(p t) o -> p (t o)", t=PACK))
        l1 = load_list("l1", n1)
        load_tab(0)
        nc.sync.dma_start(xs[0:P:8, :].bitcast(I32), x_scales[0].bitcast(I32))
        lo = load_list("lo", offs)
        nc.sync.dma_start(ga_t[:], ga.rearrange("(p t) o -> p (t o)", t=PACK))
        load_ws(0, w1_scales)
        load_ws(1, w2_scales)
        nc.sync.dma_start(xw[:].bitcast(I32), words_view(x_words))
        l2 = load_list("l2", n2)
        lt = load_list("lt", two)
        l3 = load_list("l3", n3)
        l4 = load_list("l4", n4)
        load_tab(1)
        nc.sync.dma_start(w1[:].bitcast(I32), words_view(w1_words))
        load_tab(2)
        load_tab(3)
        nc.vector.tensor_copy(xsg[:], xs[:].indirect(lo[:]))
        place_rows(xsc, xsg)
        nc.vector.tensor_copy(wsc[:].rearrange("p w (t m) -> p w m t", t=PACK), ws[:].rearrange("p w (m t) -> p w m t", t=PACK))
        for r in range(1, 4):
            nc.sync.dma_start(wsc[r:P:32].bitcast(I32), wsc[8 * r : P : 32].bitcast(I32))
        nc.sync.dma_start(w2[:].bitcast(I32), words_view(w2_words))
        l5 = load_list("l5", n5)
        l6 = load_list("l6", n6)

        for t in range(PACK):
            nc.gpsimd.tensor_scalar(tabg[t][:], tabs[t][:], ga_t[:, t : t + 1], 0.0, ALU.mult, ALU.add)
        nc.vector.tensor_copy(xg[:], xw[:].bitcast(U32).indirect(lo[:]))
        deal(w1d[:].bitcast(I32), w1[:].bitcast(I32))
        nc.vector.tensor_copy(xsg2[:], xs[:].indirect(lt[:]))
        place_rows(xsc2, xsg2)
        nc.vector.tensor_copy(xg2[:], xw[:].bitcast(U32).indirect(lt[:]))
        deal(w2d[:].bitcast(I32), w2[:].bitcast(I32))

        on_vector = ((1, 0), (2, 0), (3, 0))
        for t in range(PACK):
            for h in range(2):
                if (t, h) not in on_vector:
                    fetch(t1[:, t, h * HS : (h + 1) * HS], tabs, l1, t, h, False)
            for h in range(2):
                fetch(t2[h][:, t, :], tabg, l2, t, h, False)

        a_sb = [sb(f"a{t}", [P, S], F32) for t in range(PACK)]
        for t in range(PACK):
            product("a", t, t, w1d, 0, xg[:], xsc[:], a_sb[t][:], ga_t)
        b_sb = sb("b_sb", [P, PACK, V], F32)
        for t in range(PACK):
            product("b", 4 + t, t, w2d, 1, xg2[:], xsc2[:], b_sb[:, t, :], gb_t)
        for t, h in on_vector:
            fetch(t1[:, t, h * HS : (h + 1) * HS], tabs, l1, t, h, True)

        u = sb("u", [P, PACK, HS], F32, tag="gb_t")
        zb = sb("zb", [P, PACK, P, PACK], BF16)

        def z_piece(c0, width, tag):
            cols = slice(c0, c0 + width)
            ag = sb(f"ag{c0}", [P, PACK, width], F32, tag=tag)
            for t in range(PACK):
                nc.scalar.activation(ag[:, t, :], a_sb[t][:].indirect(entries(l3, c0, width)), ACT.Copy)
                if t % 2:
                    nc.vector.tensor_tensor(u[:, t - 1 : t + 1, 0:width], ag[:, t - 1 : t + 1, :], t1[:, t - 1 : t + 1, cols], ALU.mult)
            m = slice(c0 // PACK, (c0 + width) // PACK)
            nc.vector.tensor_tensor(
                zb[:, :, m, :].rearrange("p i c t -> p c t i"),
                u[:, :, 0:width].rearrange("p t (c i) -> p c t i", i=PACK),
                t2[c0 // HS][:, :, c0 % HS : c0 % HS + width].rearrange("p t (c i) -> p c t i", i=PACK),
                ALU.add,
            )

        def z2_all():
            z2b = sb("z2b", [P, V, PACK], BF16, tag="gb_t")
            for h in range(2):
                cols = slice(h * HV, (h + 1) * HV)
                for t in range(PACK):
                    nc.scalar.activation(bg[:, t, cols], b_sb[:, t, :].indirect(entries(l4, h * HV, HV)), ACT.Copy)
                nc.vector.tensor_tensor(
                    z2b[:, cols, :].rearrange("p (c i) t -> p c t i", i=PACK),
                    b_sb[:, :, cols].rearrange("p t (c i) -> p c t i", i=PACK),
                    bg[:, :, cols].rearrange("p t (c i) -> p c t i", i=PACK),
                    ALU.subtract,
                )
                nc.vector.quantize_mx(z2c[:, cols].bitcast(FP8X4), z2s[:, cols], z2b[:, cols, :].rearrange("p v t -> p (v t)"))

        zc = sb("zc", [P, S], U32)
        zs = sb("zs", [P, S], U8)

        def z_quant(n):
            for i in range(0, PACK, n):
                cols = slice(P * i, P * (i + n))
                nc.vector.quantize_mx(zc[:, cols].bitcast(FP8X4), zs[:, cols], zb[:, i : i + n, :, :].rearrange("p i m t -> p (i m t)"))

        bg = sb("bg", [P, PACK, V], F32)
        z2c = sb("z2c", [P, V], U32)
        z2s = sb("z2s", [P, V], U8)
        z_piece(0, 256, None)
        z_piece(256, 256, "ga_t")
        z_quant(4)
        z2_all()

        s_sb = [sb(f"s{t}", [P, V], F32) for t in range(PACK)]
        for i in range(PACK):
            cols = slice(P * i, P * (i + 1))
            acc = psum.tile([P, V], F32, name=f"acc_s{i}", tag=f"bank{4 + i}")
            nc.tensor.matmul_mx(acc[:], zc[:, cols].bitcast(FP8X4), zs[:, cols], z2c[:].bitcast(FP8X4), z2s[:], start=True, stop=True)
            nc.vector.tensor_scalar(s_sb[i][:], acc[:], 0.0625, None, ALU.mult)
        sg = sb("sg", [P, PACK, V], F32)
        st = sb("st", [P, PACK, V], F32)
        for i in range(PACK):
            for h in range(2):
                nc.scalar.activation(sg[:, i, h * HV : (h + 1) * HV], s_sb[i][:].indirect(entries(l5, h * HV, HV)), ACT.Sigmoid)
        for i in range(PACK):
            nc.vector.tensor_tensor(st[:, i, :], s_sb[i][:], sg[:, i, :], ALU.mult)

        stg = sb("stg", [P, PACK, V], F32)
        o = sb("o", [P, PACK, V], F32)
        ob = sb("ob", [P, V, PACK], BF16)
        oc = sb("oc", [P, V], U32)
        osc = sb("osc", [P, V], U8)
        out_v = out_0.rearrange("(p t) v -> p t v", t=PACK)
        halves = [slice(0, HV), slice(HV, V)]
        for i in range(PACK):
            for h in range(2):
                nc.scalar.activation(stg[:, i, halves[h]], st[:, i, :].indirect(entries(l6, h * HV, HV)), ACT.Copy)
            for cols in (halves if i == PACK - 1 else [slice(0, V)]):
                nc.vector.tensor_tensor(o[:, i, cols], st[:, i, cols], stg[:, i, cols], ALU.subtract)
            nc.sync.dma_start(out_v[:, i, :], o[:, i, :])
        for cols in halves:
            nc.vector.tensor_copy(
                ob[:, cols, :].rearrange("p (c i) t -> p c t i", i=PACK),
                o[:, :, cols].rearrange("p t (c i) -> p c t i", i=PACK),
            )
        for cols in halves:
            nc.vector.quantize_mx(oc[:, cols].bitcast(FP8X4), osc[:, cols], ob[:, cols, :].rearrange("p v t -> p (v t)"))
        nc.sync.dma_start(words_view(out_1), oc[:].bitcast(I32))
        for q in range(4):
            eng = nc.sync if q == 3 else nc.scalar
            eng.dma_start(out_2[0, 4 * q : 4 * q + 4, :].bitcast(I32), osc[32 * q : 32 * q + 4, :].bitcast(I32))
